import numpy as np
import ml_dtypes

BF16 = ml_dtypes.bfloat16


def bf(x):
    return np.asarray(x, np.float32).astype(BF16)


def f32(x):
    return np.asarray(x, np.float32)


def f64(x):
    return np.asarray(x).astype(np.float64)


def striped(idx):
    return np.tile(idx.reshape(-1, 16).T, (8, 1))


S, K, M, N, E, Q = 512, 512, 128, 128, 2, 64


def setup_inputs():
    return {"base": bf(np.random.standard_normal((M, S))), "x": bf(np.random.standard_normal((K, N))), "w": bf(np.random.standard_normal((E, K, M)) / np.sqrt(K)), "s": f32(0.5 + np.random.random_sample((M, 1))), "b": f32(0.5 * np.random.standard_normal((M, 1))), "offs": striped(np.random.permutation(S)[:N])}


def reference(base, x, w, s, b, offs):
    idx = offs[:16].T.reshape(-1)
    z = f64(base).copy()
    for e in range(E):
        z[:, idx[e * Q : (e + 1) * Q]] += f64(w)[e].T @ f64(x)[:, e * Q : (e + 1) * Q]
    return z * f64(s) + f64(b)

@@ -1,0 +1,57 @@
+import concourse.mybir as mybir
+from concourse.masks import make_identity
+
+P = 128
+S = 512
+K = 512
+KB = K // P
+N = 128
+E = 2
+Q = N // E
+QC = Q // 16
+
+BF16, F32, U16 = mybir.dt.bfloat16, mybir.dt.float32, mybir.dt.uint16
+MULT, ADD = mybir.AluOpType.mult, mybir.AluOpType.add
+
+FLOPS = 2 * K * P * N
+
+
+def tile_scatter_matmul_kernel(tc, base, x, w, s, b, offs, out):
+    nc = tc.nc
+    with (
+        tc.tile_pool(name="held", bufs=1) as held,
+        tc.psum_pool(name="psum", bufs=1) as psum,
+    ):
+        offsets = held.tile([P, N // 16], U16, name="offsets")
+        base_sb = held.tile([P, S], BF16, name="base_sb")
+        x_sb = held.tile([P, KB, N], BF16, name="x_sb")
+        w_sb = held.tile([P, E, KB, P], BF16, name="w_sb")
+        gain = held.tile([P, 1], F32, name="gain")
+        shift = held.tile([P, 1], F32, name="shift")
+        ident = held.tile([P, P], BF16, name="ident")
+        result = held.tile([P, S], F32, name="result")
+        window = psum.tile([P, S], F32, name="window")
+
+        nc.sync.dma_start(offsets[:], offs)
+        nc.scalar.dma_start(base_sb[:], base)
+        nc.sync.dma_start(w_sb[:], w.rearrange("e (p a) m -> p e a m", a=KB))
+        nc.scalar.dma_start(x_sb[:], x.rearrange("(p a) n -> p a n", a=KB))
+        nc.gpsimd.dma_start(gain[:], s)
+        nc.gpsimd.dma_start(shift[:], b)
+        make_identity(nc, ident[:])
+
+        nc.tensor.matmul(window[:], ident[:], base_sb[:], start=True, stop=False)
+
+        for e in range(E):
+            places = window[:].indirect(offsets[:, e * QC : (e + 1) * QC])
+            for a in range(KB):
+                nc.tensor.matmul(
+                    places,
+                    w_sb[:, e, a, :],
+                    x_sb[:, a, e * Q : (e + 1) * Q],
+                    start=False,
+                    stop=(e == E - 1 and a == KB - 1),
+                )
+
+        nc.vector.tensor_scalar(result[:], window[:], gain[:, 0:1], shift[:, 0:1], MULT, ADD)
+        nc.sync.dma_start(out, result[:])

@@ -25,20 +25,21 @@ def tile_scatter_matmul_kernel(tc, base, x, w, s, b, offs, out):
         offsets = held.tile([P, N // 16], U16, name="offsets")
         base_sb = held.tile([P, S], BF16, name="base_sb")
         x_sb = held.tile([P, KB, N], BF16, name="x_sb")
-        w_sb = held.tile([P, E, KB, P], BF16, name="w_sb")
+        w_sb = [held.tile([P, KB, P], BF16, name=f"w_sb{e}") for e in range(E)]
         gain = held.tile([P, 1], F32, name="gain")
         shift = held.tile([P, 1], F32, name="shift")
         ident = held.tile([P, P], BF16, name="ident")
         result = held.tile([P, S], F32, name="result")
         window = psum.tile([P, S], F32, name="window")
 
+        make_identity(nc, ident[:])
         nc.sync.dma_start(offsets[:], offs)
         nc.scalar.dma_start(base_sb[:], base)
-        nc.sync.dma_start(w_sb[:], w.rearrange("e (p a) m -> p e a m", a=KB))
-        nc.scalar.dma_start(x_sb[:], x.rearrange("(p a) n -> p a n", a=KB))
-        nc.gpsimd.dma_start(gain[:], s)
-        nc.gpsimd.dma_start(shift[:], b)
-        make_identity(nc, ident[:])
+        nc.sync.dma_start(x_sb[:], x.rearrange("(p a) n -> p a n", a=KB))
+        nc.scalar.dma_start(w_sb[0][:], w[0].rearrange("(p a) m -> p a m", a=KB))
+        nc.sync.dma_start(w_sb[1][:], w[1].rearrange("(p a) m -> p a m", a=KB))
+        nc.scalar.dma_start(gain[:], s)
+        nc.sync.dma_start(shift[:], b)
 
         nc.tensor.matmul(window[:], ident[:], base_sb[:], start=True, stop=False)
 
@@ -47,7 +48,7 @@ def tile_scatter_matmul_kernel(tc, base, x, w, s, b, offs, out):
             for a in range(KB):
                 nc.tensor.matmul(
                     places,
-                    w_sb[:, e, a, :],
+                    w_sb[e][:, a, :],
                     x_sb[:, a, e * Q : (e + 1) * Q],
                     start=False,
                     stop=(e == E - 1 and a == KB - 1),

@@ -8,6 +8,8 @@ KB = K // P
 N = 128
 E = 2
 Q = N // E
+WARM_MATMULS = 3
+WARM_COLS = 512
 QC = Q // 16
 
 BF16, F32, U16 = mybir.dt.bfloat16, mybir.dt.float32, mybir.dt.uint16
@@ -31,6 +33,12 @@ def tile_scatter_matmul_kernel(tc, base, x, w, s, b, offs, out):
         ident = held.tile([P, P], BF16, name="ident")
         result = held.tile([P, S], F32, name="result")
         window = psum.tile([P, S], F32, name="window")
+        zeros = held.tile([P, WARM_COLS], BF16, name="zeros")
+        unused = psum.tile([P, WARM_COLS], F32, name="unused")
+
+        nc.vector.memset(zeros[:].bitcast(F32), 0.0)
+        for i in range(WARM_MATMULS):
+            nc.tensor.matmul(unused[:], zeros[:, 0:P], zeros[:], start=True, stop=True)
 
         make_identity(nc, ident[:])
         nc.sync.dma_start(offsets[:], offs)

@@ -41,12 +41,12 @@ def tile_scatter_matmul_kernel(tc, base, x, w, s, b, offs, out):
             nc.tensor.matmul(unused[:], zeros[:, 0:P], zeros[:], start=True, stop=True)
 
         make_identity(nc, ident[:])
+        nc.sync.dma_start(base_sb[:], base)
         nc.sync.dma_start(offsets[:], offs)
-        nc.scalar.dma_start(base_sb[:], base)
         nc.sync.dma_start(x_sb[:], x.rearrange("(p a) n -> p a n", a=KB))
-        nc.scalar.dma_start(w_sb[0][:], w[0].rearrange("(p a) m -> p a m", a=KB))
+        nc.sync.dma_start(w_sb[0][:], w[0].rearrange("(p a) m -> p a m", a=KB))
         nc.sync.dma_start(w_sb[1][:], w[1].rearrange("(p a) m -> p a m", a=KB))
-        nc.scalar.dma_start(gain[:], s)
+        nc.sync.dma_start(gain[:], s)
         nc.sync.dma_start(shift[:], b)
 
         nc.tensor.matmul(window[:], ident[:], base_sb[:], start=True, stop=False)

@@ -11,6 +11,7 @@ Q = N // E
 WARM_MATMULS = 3
 WARM_COLS = 512
 QC = Q // 16
+TB = 32
 
 BF16, F32, U16 = mybir.dt.bfloat16, mybir.dt.float32, mybir.dt.uint16
 MULT, ADD = mybir.AluOpType.mult, mybir.AluOpType.add
@@ -28,8 +29,8 @@ def tile_scatter_matmul_kernel(tc, base, x, w, s, b, offs, out):
         base_sb = held.tile([P, S], BF16, name="base_sb")
         x_sb = held.tile([P, KB, N], BF16, name="x_sb")
         w_sb = [held.tile([P, KB, P], BF16, name=f"w_sb{e}") for e in range(E)]
-        gain = held.tile([P, 1], F32, name="gain")
-        shift = held.tile([P, 1], F32, name="shift")
+        as_rows = held.tile([P, 2 * TB], F32, name="as_rows", align_bytes=64)
+        as_columns = held.tile([P, 2 * TB], F32, name="as_columns", align_bytes=64)
         ident = held.tile([P, P], BF16, name="ident")
         result = held.tile([P, S], F32, name="result")
         window = psum.tile([P, S], F32, name="window")
@@ -37,6 +38,7 @@ def tile_scatter_matmul_kernel(tc, base, x, w, s, b, offs, out):
         unused = psum.tile([P, WARM_COLS], F32, name="unused")
 
         nc.vector.memset(zeros[:].bitcast(F32), 0.0)
+        nc.vector.memset(as_rows[:], 0.0)
         for i in range(WARM_MATMULS):
             nc.tensor.matmul(unused[:], zeros[:, 0:P], zeros[:], start=True, stop=True)
 
@@ -46,8 +48,11 @@ def tile_scatter_matmul_kernel(tc, base, x, w, s, b, offs, out):
         nc.sync.dma_start(x_sb[:], x.rearrange("(p a) n -> p a n", a=KB))
         nc.sync.dma_start(w_sb[0][:], w[0].rearrange("(p a) m -> p a m", a=KB))
         nc.sync.dma_start(w_sb[1][:], w[1].rearrange("(p a) m -> p a m", a=KB))
-        nc.sync.dma_start(gain[:], s)
-        nc.sync.dma_start(shift[:], b)
+        for j, vector in enumerate((s, b)):
+            block = slice(j * TB, (j + 1) * TB)
+            nc.sync.dma_start(as_rows[0:P:TB, block], vector.rearrange("(g i) o -> g (i o)", i=TB))
+            nc.vector.transpose(as_columns[:, block], as_rows[:, block])
+        gain, shift = as_columns[:, 0:1], as_columns[:, TB : TB + 1]
 
         nc.tensor.matmul(window[:], ident[:], base_sb[:], start=True, stop=False)
 
@@ -62,5 +67,5 @@ def tile_scatter_matmul_kernel(tc, base, x, w, s, b, offs, out):
                     stop=(e == E - 1 and a == KB - 1),
                 )
 
-        nc.vector.tensor_scalar(result[:], window[:], gain[:, 0:1], shift[:, 0:1], MULT, ADD)
+        nc.vector.tensor_scalar(result[:], window[:], gain, shift, MULT, ADD)
         nc.sync.dma_start(out, result[:])

@@ -12,6 +12,7 @@ WARM_MATMULS = 3
 WARM_COLS = 512
 QC = Q // 16
 TB = 32
+AXI = 256
 
 BF16, F32, U16 = mybir.dt.bfloat16, mybir.dt.float32, mybir.dt.uint16
 MULT, ADD = mybir.AluOpType.mult, mybir.AluOpType.add
@@ -26,13 +27,13 @@ def tile_scatter_matmul_kernel(tc, base, x, w, s, b, offs, out):
         tc.psum_pool(name="psum", bufs=1) as psum,
     ):
         offsets = held.tile([P, N // 16], U16, name="offsets")
-        base_sb = held.tile([P, S], BF16, name="base_sb")
-        x_sb = held.tile([P, KB, N], BF16, name="x_sb")
-        w_sb = [held.tile([P, KB, P], BF16, name=f"w_sb{e}") for e in range(E)]
+        base_sb = held.tile([P, S], BF16, name="base_sb", align_bytes=AXI)
+        x_sb = held.tile([P, KB, N], BF16, name="x_sb", align_bytes=AXI)
+        w_sb = [held.tile([P, KB, P], BF16, name=f"w_sb{e}", align_bytes=AXI) for e in range(E)]
         as_rows = held.tile([P, 2 * TB], F32, name="as_rows", align_bytes=64)
         as_columns = held.tile([P, 2 * TB], F32, name="as_columns", align_bytes=64)
         ident = held.tile([P, P], BF16, name="ident")
-        result = held.tile([P, S], F32, name="result")
+        result = held.tile([P, S], F32, name="result", align_bytes=AXI)
         window = psum.tile([P, S], F32, name="window")
         zeros = held.tile([P, WARM_COLS], BF16, name="zeros")
         unused = psum.tile([P, WARM_COLS], F32, name="unused")

@@ -12,7 +12,7 @@ WARM_MATMULS = 3
 WARM_COLS = 512
 QC = Q // 16
 TB = 32
-AXI = 256
+ROW = 2 * S
 
 BF16, F32, U16 = mybir.dt.bfloat16, mybir.dt.float32, mybir.dt.uint16
 MULT, ADD = mybir.AluOpType.mult, mybir.AluOpType.add
@@ -27,13 +27,13 @@ def tile_scatter_matmul_kernel(tc, base, x, w, s, b, offs, out):
         tc.psum_pool(name="psum", bufs=1) as psum,
     ):
         offsets = held.tile([P, N // 16], U16, name="offsets")
-        base_sb = held.tile([P, S], BF16, name="base_sb", align_bytes=AXI)
-        x_sb = held.tile([P, KB, N], BF16, name="x_sb", align_bytes=AXI)
-        w_sb = [held.tile([P, KB, P], BF16, name=f"w_sb{e}", align_bytes=AXI) for e in range(E)]
+        base_sb = held.tile([P, S], BF16, name="base_sb", align_bytes=ROW)
+        x_sb = held.tile([P, KB, N], BF16, name="x_sb", align_bytes=ROW)
+        w_sb = [held.tile([P, KB, P], BF16, name=f"w_sb{e}", align_bytes=ROW) for e in range(E)]
         as_rows = held.tile([P, 2 * TB], F32, name="as_rows", align_bytes=64)
         as_columns = held.tile([P, 2 * TB], F32, name="as_columns", align_bytes=64)
         ident = held.tile([P, P], BF16, name="ident")
-        result = held.tile([P, S], F32, name="result", align_bytes=AXI)
+        result = held.tile([P, S], F32, name="result", align_bytes=2 * ROW)
         window = psum.tile([P, S], F32, name="window")
         zeros = held.tile([P, WARM_COLS], BF16, name="zeros")
         unused = psum.tile([P, WARM_COLS], F32, name="unused")

@@ -8,8 +8,9 @@ KB = K // P
 N = 128
 E = 2
 Q = N // E
-WARM_MATMULS = 3
+WARM_ROUNDS = 3
 WARM_COLS = 512
+CT = 32
 QC = Q // 16
 TB = 32
 ROW = 2 * S
@@ -40,8 +41,9 @@ def tile_scatter_matmul_kernel(tc, base, x, w, s, b, offs, out):
 
         nc.vector.memset(zeros[:].bitcast(F32), 0.0)
         nc.vector.memset(as_rows[:], 0.0)
-        for i in range(WARM_MATMULS):
-            nc.tensor.matmul(unused[:], zeros[:, 0:P], zeros[:], start=True, stop=True)
+        for i in range(WARM_ROUNDS):
+            for first in range(0, P, CT):
+                nc.tensor.matmul(unused[first : first + CT, :], zeros[:, 0:CT], zeros[:], start=True, stop=True)
 
         make_identity(nc, ident[:])
         nc.sync.dma_start(base_sb[:], base)

@@ -70,5 +70,5 @@ def tile_scatter_matmul_kernel(tc, base, x, w, s, b, offs, out):
                     stop=(e == E - 1 and a == KB - 1),
                 )
 
-        nc.vector.tensor_scalar(result[:], window[:], gain, shift, MULT, ADD)
+        nc.vector.scalar_tensor_tensor(result[:], window[:], gain, shift.to_broadcast([P, S]), MULT, ADD)
         nc.sync.dma_start(out, result[:])

@@ -36,14 +36,15 @@ def tile_scatter_matmul_kernel(tc, base, x, w, s, b, offs, out):
         ident = held.tile([P, P], BF16, name="ident")
         result = held.tile([P, S], F32, name="result", align_bytes=2 * ROW)
         window = psum.tile([P, S], F32, name="window")
-        zeros = held.tile([P, WARM_COLS], BF16, name="zeros")
+        zeros = held.tile([P, CT], BF16, name="zeros")
         unused = psum.tile([P, WARM_COLS], F32, name="unused")
 
-        nc.vector.memset(zeros[:].bitcast(F32), 0.0)
+        nc.gpsimd.memset(zeros[:].bitcast(F32), 0.0)
         nc.vector.memset(as_rows[:], 0.0)
+        zeros_again = zeros[:].unsqueeze(1).to_broadcast([P, WARM_COLS // CT, CT])
         for i in range(WARM_ROUNDS):
             for first in range(0, P, CT):
-                nc.tensor.matmul(unused[first : first + CT, :], zeros[:, 0:CT], zeros[:], start=True, stop=True)
+                nc.tensor.matmul(unused[first : first + CT, :], zeros[:], zeros_again, start=True, stop=True)
 
         make_identity(nc, ident[:])
         nc.sync.dma_start(base_sb[:], base)

@@ -1,5 +1,4 @@
 import concourse.mybir as mybir
-from concourse.masks import make_identity
 
 P = 128
 S = 512
@@ -16,7 +15,7 @@ TB = 32
 ROW = 2 * S
 
 BF16, F32, U16 = mybir.dt.bfloat16, mybir.dt.float32, mybir.dt.uint16
-MULT, ADD = mybir.AluOpType.mult, mybir.AluOpType.add
+MULT, ADD, IS_EQUAL = mybir.AluOpType.mult, mybir.AluOpType.add, mybir.AluOpType.is_equal
 
 FLOPS = 2 * K * P * N
 
@@ -34,24 +33,34 @@ def tile_scatter_matmul_kernel(tc, base, x, w, s, b, offs, out):
         as_rows = held.tile([P, 2 * TB], F32, name="as_rows", align_bytes=64)
         as_columns = held.tile([P, 2 * TB], F32, name="as_columns", align_bytes=64)
         ident = held.tile([P, P], BF16, name="ident")
+        ones = held.tile([P, TB], F32, name="ones", align_bytes=64)
+        ramp = held.tile([P, TB], F32, name="ramp", align_bytes=64)
+        ramp_turned = held.tile([P, TB], F32, name="ramp_turned", align_bytes=64)
         result = held.tile([P, S], F32, name="result", align_bytes=2 * ROW)
         window = psum.tile([P, S], F32, name="window")
         zeros = held.tile([P, CT], BF16, name="zeros")
         unused = psum.tile([P, WARM_COLS], F32, name="unused")
 
-        nc.gpsimd.memset(zeros[:].bitcast(F32), 0.0)
-        nc.vector.memset(as_rows[:], 0.0)
+        nc.vector.memset(zeros[:].bitcast(F32), 0.0)
         zeros_again = zeros[:].unsqueeze(1).to_broadcast([P, WARM_COLS // CT, CT])
         for i in range(WARM_ROUNDS):
             for first in range(0, P, CT):
                 nc.tensor.matmul(unused[first : first + CT, :], zeros[:], zeros_again, start=True, stop=True)
 
-        make_identity(nc, ident[:])
         nc.sync.dma_start(base_sb[:], base)
         nc.sync.dma_start(offsets[:], offs)
         nc.sync.dma_start(x_sb[:], x.rearrange("(p a) n -> p a n", a=KB))
         nc.sync.dma_start(w_sb[0][:], w[0].rearrange("(p a) m -> p a m", a=KB))
         nc.sync.dma_start(w_sb[1][:], w[1].rearrange("(p a) m -> p a m", a=KB))
+        nc.vector.memset(ones[:], 1.0)
+        nc.vector.tensor_tensor_scan(ramp[:], ones[:], ones[:], 0.0, MULT, ADD)
+        nc.vector.transpose(ramp_turned[:], ramp[:])
+        nc.vector.memset(ident[:].bitcast(F32), 0.0)
+        for g in range(P // TB):
+            own = slice(g * TB, (g + 1) * TB)
+            nc.vector.tensor_tensor(ident[own, own], ramp[own, :], ramp_turned[own, :], IS_EQUAL)
+        nc.vector.memset(as_rows[:], 0.0)
+
         for j, vector in enumerate((s, b)):
             block = slice(j * TB, (j + 1) * TB)
             nc.sync.dma_start(as_rows[0:P:TB, block], vector.rearrange("(g i) o -> g (i o)", i=TB))

@@ -38,14 +38,15 @@ def tile_scatter_matmul_kernel(tc, base, x, w, s, b, offs, out):
         ramp_turned = held.tile([P, TB], F32, name="ramp_turned", align_bytes=64)
         result = held.tile([P, S], F32, name="result", align_bytes=2 * ROW)
         window = psum.tile([P, S], F32, name="window")
-        zeros = held.tile([P, CT], BF16, name="zeros")
+        signs = held.tile([P, CT], BF16, name="signs")
         unused = psum.tile([P, WARM_COLS], F32, name="unused")
 
-        nc.vector.memset(zeros[:].bitcast(F32), 0.0)
-        zeros_again = zeros[:].unsqueeze(1).to_broadcast([P, WARM_COLS // CT, CT])
+        nc.vector.memset(signs[:, 0:CT:2], 1.0)
+        nc.vector.memset(signs[:, 1:CT:2], -1.0)
+        signs_again = signs[:].unsqueeze(1).to_broadcast([P, WARM_COLS // CT, CT])
         for i in range(WARM_ROUNDS):
             for first in range(0, P, CT):
-                nc.tensor.matmul(unused[first : first + CT, :], zeros[:], zeros_again, start=True, stop=True)
+                nc.tensor.matmul(unused[first : first + CT, :], signs[:], signs_again, start=True, stop=True)
 
         nc.sync.dma_start(base_sb[:], base)
         nc.sync.dma_start(offsets[:], offs)

import concourse.mybir as mybir

P = 128
S = 512
K = 512
KB = K // P
N = 128
E = 2
Q = N // E
WARM_ROUNDS = 3
WARM_COLS = 512
CT = 32
QC = Q // 16
TB = 32
ROW = 2 * S

BF16, F32, U16 = mybir.dt.bfloat16, mybir.dt.float32, mybir.dt.uint16
MULT, ADD, IS_EQUAL = mybir.AluOpType.mult, mybir.AluOpType.add, mybir.AluOpType.is_equal

FLOPS = 2 * K * P * N


def tile_scatter_matmul_kernel(tc, base, x, w, s, b, offs, out):
    nc = tc.nc
    with (
        tc.tile_pool(name="held", bufs=1) as held,
        tc.psum_pool(name="psum", bufs=1) as psum,
    ):
        offsets = held.tile([P, N // 16], U16, name="offsets")
        base_sb = held.tile([P, S], BF16, name="base_sb", align_bytes=ROW)
        x_sb = held.tile([P, KB, N], BF16, name="x_sb", align_bytes=ROW)
        w_sb = [held.tile([P, KB, P], BF16, name=f"w_sb{e}", align_bytes=ROW) for e in range(E)]
        as_rows = held.tile([P, 2 * TB], F32, name="as_rows", align_bytes=64)
        as_columns = held.tile([P, 2 * TB], F32, name="as_columns", align_bytes=64)
        ident = held.tile([P, P], BF16, name="ident")
        ones = held.tile([P, TB], F32, name="ones", align_bytes=64)
        ramp = held.tile([P, TB], F32, name="ramp", align_bytes=64)
        ramp_turned = held.tile([P, TB], F32, name="ramp_turned", align_bytes=64)
        result = held.tile([P, S], F32, name="result", align_bytes=2 * ROW)
        window = psum.tile([P, S], F32, name="window")
        signs = held.tile([P, CT], BF16, name="signs")
        unused = psum.tile([P, WARM_COLS], F32, name="unused")

        nc.vector.memset(signs[:, 0:CT:2], 1.0)
        nc.vector.memset(signs[:, 1:CT:2], -1.0)
        signs_again = signs[:].unsqueeze(1).to_broadcast([P, WARM_COLS // CT, CT])
        for i in range(WARM_ROUNDS):
            for first in range(0, P, CT):
                nc.tensor.matmul(unused[first : first + CT, :], signs[:], signs_again, start=True, stop=True)

        nc.sync.dma_start(base_sb[:], base)
        nc.sync.dma_start(offsets[:], offs)
        nc.sync.dma_start(x_sb[:], x.rearrange("(p a) n -> p a n", a=KB))
        nc.sync.dma_start(w_sb[0][:], w[0].rearrange("(p a) m -> p a m", a=KB))
        nc.sync.dma_start(w_sb[1][:], w[1].rearrange("(p a) m -> p a m", a=KB))
        nc.vector.memset(ones[:], 1.0)
        nc.vector.tensor_tensor_scan(ramp[:], ones[:], ones[:], 0.0, MULT, ADD)
        nc.vector.transpose(ramp_turned[:], ramp[:])
        nc.vector.memset(ident[:].bitcast(F32), 0.0)
        for g in range(P // TB):
            own = slice(g * TB, (g + 1) * TB)
            nc.vector.tensor_tensor(ident[own, own], ramp[own, :], ramp_turned[own, :], IS_EQUAL)
        nc.vector.memset(as_rows[:], 0.0)

        for j, vector in enumerate((s, b)):
            block = slice(j * TB, (j + 1) * TB)
            nc.sync.dma_start(as_rows[0:P:TB, block], vector.rearrange("(g i) o -> g (i o)", i=TB))
            nc.vector.transpose(as_columns[:, block], as_rows[:, block])
        gain, shift = as_columns[:, 0:1], as_columns[:, TB : TB + 1]

        nc.tensor.matmul(window[:], ident[:], base_sb[:], start=True, stop=False)

        for e in range(E):
            places = window[:].indirect(offsets[:, e * QC : (e + 1) * QC])
            for a in range(KB):
                nc.tensor.matmul(
                    places,
                    w_sb[e][:, a, :],
                    x_sb[:, a, e * Q : (e + 1) * Q],
                    start=False,
                    stop=(e == E - 1 and a == KB - 1),
                )

        nc.vector.scalar_tensor_tensor(result[:], window[:], gain, shift.to_broadcast([P, S]), MULT, ADD)
        nc.sync.dma_start(out, result[:])
